import numpy as np
CORES = [2,10,130,138,258,266,386,394]
N = 8
T, K = 16, 2
ROUTE = [[[1,6],[0,3],[2,0],[0,1],[5,0],[0,2],[4,5],[1,6],[7,5],[2,7],[7,1],[7,1],[6,3],[5,7],[4,2],[1,5]],[[1,5],[7,6],[2,6],[4,5],[3,1],[3,5],[1,4],[1,5],[2,5],[2,3],[1,6],[1,5],[2,0],[2,4],[6,0],[0,3]],[[3,5],[1,6],[7,2],[2,6],[4,7],[6,2],[6,4],[6,2],[6,0],[1,0],[3,1],[6,5],[4,5],[0,6],[3,4],[6,7]],[[4,0],[3,0],[5,6],[4,0],[7,0],[5,4],[6,0],[1,2],[3,0],[5,4],[2,0],[0,6],[1,3],[1,5],[0,6],[2,3]],[[0,5],[2,7],[4,6],[2,4],[1,2],[5,3],[4,5],[5,1],[7,4],[3,6],[7,6],[6,2],[1,3],[6,2],[2,1],[6,0]],[[5,1],[3,5],[1,0],[2,3],[4,5],[7,4],[6,7],[2,3],[5,4],[6,5],[5,3],[2,5],[0,3],[7,0],[2,5],[1,2]],[[4,1],[7,3],[0,2],[3,2],[2,3],[5,1],[0,3],[5,7],[4,3],[6,4],[6,5],[5,1],[5,1],[3,6],[2,1],[1,2]],[[3,0],[4,5],[6,5],[4,1],[0,2],[5,4],[6,0],[0,6],[3,4],[6,4],[7,4],[4,0],[6,4],[0,1],[2,5],[0,2]]]
ZW = 39
def setup_inputs(rng):
    return {"z": rng.standard_normal((N, 128, ZW), dtype=np.float32), "g": rng.random((N, 128, T * K), dtype=np.float32)}
def reference(z, g):
    y = np.zeros((N, 128, T), np.float64)
    fill = [0] * N
    for r in range(N):
        for t in range(T):
            for k, e in enumerate(ROUTE[r][t]):
                y[r][:, t] += g[r][:, t * K + k].astype(np.float64) * z[e][:, fill[e]].astype(np.float64)
                fill[e] += 1
    return {"y": y.astype(z.dtype)}

@@ -1,0 +1,222 @@
+import concourse.bass as bass
+import concourse.mybir as mybir
+
+LW = 52
+SCRATCH = {
+    "zs": ("sbuf", [128, 40], "float32"),
+    "gs": ("sbuf", [128, 32], "float32"),
+    "land": ("sbuf", [128, LW], "float32"),
+    "gp": ("sbuf", [128, LW], "float32"),
+    "prod": ("sbuf", [128, LW], "float32"),
+    "yb": ("sbuf", [128, 16], "float32"),
+}
+SEMAPHORES = ["zl", "gl", "st", "vs", "sent", "si", "rx", "cx", "mt", "rs", "cs", "d0", "d1"]
+
+STAGES = [["rx", "cx"], ["mt", "rs"], ["cs"], ["d0", "d1"]]
+R_CORE, A_CORE = 3, 6
+
+
+def ap_groups(items):
+    left = sorted(items)
+    out = []
+    while left:
+        have = set(left)
+        best = [left[0]]
+        for p in left:
+            for q in left:
+                if q[0] > p[0] and q[1] > p[1]:
+                    da, db = q[0] - p[0], q[1] - p[1]
+                    run = [p, q]
+                    nxt = (q[0] + da, q[1] + db)
+                    while nxt in have:
+                        run.append(nxt)
+                        nxt = (nxt[0] + da, nxt[1] + db)
+                    if len(run) > len(best):
+                        best = run
+        if len(best) == 1:
+            sa, sb = slice(best[0][0], best[0][0] + 1), slice(best[0][1], best[0][1] + 1)
+        else:
+            da, db = best[1][0] - best[0][0], best[1][1] - best[0][1]
+            sa, sb = slice(best[0][0], best[-1][0] + 1, da), slice(best[0][1], best[-1][1] + 1, db)
+        out.append((sa, sb, [p[0] for p in best]))
+        left = [p for p in left if p not in best]
+    return out
+
+
+def kind_of(he, ce, hr, cr):
+    if he == hr:
+        return "self" if ce == cr else "mt"
+    if hr == he ^ 1:
+        return "rs" if ce == cr else "rx"
+    if hr == 3 - he:
+        return "cs" if ce == cr else "cx"
+    return "d0" if ce == 0 else "d1"
+
+
+def make_plan(tables, cores, topo):
+    route, zw = tables["ROUTE"], tables["ZW"]
+    n = len(route)
+    place = [(topo.host(c), topo.chip(c)) for c in cores]
+    cols = [[[] for r in range(n)] for e in range(n)]
+    off = [[0] * n for e in range(n)]
+    fill = [0] * n
+    for r in range(n):
+        for e in range(n):
+            off[e][r] = fill[e]
+        for t, ex in enumerate(route[r]):
+            for k, e in enumerate(ex):
+                cols[e][r].append((t, k))
+                fill[e] += 1
+    cnt = [[len(cols[e][r]) for r in range(n)] for e in range(n)]
+    kind = [[kind_of(place[e][0], place[e][1], place[r][0], place[r][1]) for r in range(n)] for e in range(n)]
+
+    win, chunk = {}, {}
+    for e in range(n):
+        to = {kind[e][r]: r for r in range(n)}
+        dd = [r for r in range(n) if kind[e][r] in ("d0", "d1")]
+        via_r, via_a, direct = dd + [to["cs"]], [to["mt"], to["rs"]], [to["rx"], to["cx"]]
+        lo_r, hi_r = min(off[e][r] for r in via_r), max(off[e][r] + cnt[e][r] for r in via_r)
+        lo_a, hi_a = min(off[e][r] for r in via_a), max(off[e][r] + cnt[e][r] for r in via_a)
+        w1 = max(hi_r - lo_r, hi_a - lo_a)
+        s_r, s_a = min(lo_r, zw - w1), min(lo_a, zw - w1)
+        chunk[e] = (s_r, s_a, w1, via_r, via_a, direct)
+        for grp, lo, hi in ((via_r, s_r, s_r + w1), (via_a, s_a, s_a + w1), (direct, 0, zw)):
+            w = max(cnt[e][r] for r in grp)
+            for r in grp:
+                win[(e, r)] = (min(off[e][r], hi - w), w)
+
+    col = [[0] * n for r in range(n)]
+    base = [[0] * n for r in range(n)]
+    span = [{} for r in range(n)]
+    for r in range(n):
+        frm = {kind[e][r]: e for e in range(n)}
+        at = cnt[r][r]
+        span[r]["self"] = (0, at)
+        for st in STAGES:
+            for kd in st:
+                e = frm[kd]
+                ws, w = win[(e, r)]
+                base[r][e], col[r][e] = at, at + off[e][r] - ws
+                span[r][kd] = (at, at + w)
+                at += w
+        assert at <= LW
+
+    calls = {}
+    for e in range(n):
+        s = cores[e]
+        he, ce = place[e]
+        rc = (3 - he) * 128 + ce * 8 + R_CORE
+        ac = he * 128 + ce * 8 + A_CORE
+        s_r, s_a, w1, via_r, via_a, direct = chunk[e]
+
+        def last(buf, shift, grp, masks):
+            return [(buf, win[(e, r)][0] - shift, win[(e, r)][1], cores[r], base[r][e], m, kind[e][r])
+                    for r, m in zip(grp, masks) if cnt[e][r]]
+
+        calls[s] = [(0, [("zs", s_r, w1, rc, 0, 0x00FF, "si"), ("zs", s_a, w1, ac, 0, 0xFF00, "si")]),
+                    (0, last("zs", 0, direct, (0x0F, 0xF0)))]
+        calls[rc] = [(8, last("land", s_r, via_r, (0x0F, 0xF0, 0xFF00)))]
+        calls[ac] = [(8, last("land", s_a, via_a, (0x0F, 0xF0)))]
+    return calls, cols, cnt, off, kind, col, span
+
+
+def engines(mask):
+    return bin(mask).count("1")
+
+
+def issue(g, core, T, topo, call_list):
+    sems = {"si": T.sem.si, "rx": T.sem.rx, "cx": T.sem.cx, "mt": T.sem.mt, "rs": T.sem.rs, "cs": T.sem.cs,
+            "d0": T.sem.d0, "d1": T.sem.d1}
+    bufs = {"zs": T.zs, "land": T.land}
+    left = 0
+    for need, trs in call_list:
+        if need:
+            g.wait_ge(T.sem.si, need)
+        if not trs:
+            continue
+        lst = []
+        for buf, lo, w, dst, dlo, mask, sem in trs:
+            rid, pid = topo.addr(dst, core)
+            assert mask & ~topo.mask(core, dst) == 0
+            lst.append(bass.RemoteDMATransfer(dst_ids=[bass.DstId(rid=rid, pnc=pid)], dma_engine_mask=mask,
+                                              remote_sem=sems[sem], src=bufs[buf][:, lo:lo + w],
+                                              dst=T.land[:, dlo:dlo + w]))
+            left += engines(mask)
+        g.remote_dma_fused(lst, local_sem=T.sem.sent)
+    if left:
+        g.wait_ge(T.sem.sent, left)
+
+
+def rank_program(g, core, T, topo):
+    calls, cols, cnt, off, kind, col, span = make_plan(T.tables, T.cores, topo)
+    rank = T.rank_of(core)
+    if rank is None:
+        if core in calls:
+            issue(g, core, T, topo, calls[core])
+        return
+    n, kk, zw = len(T.cores), T.tables["K"], T.tables["ZW"]
+    add, mult = mybir.AluOpType.add, mybir.AluOpType.mult
+    v = g.vector
+
+    g.sync.dma_start(out=T.zs[:, 0:zw], in_=T.z[:]).then_inc(T.sem.zl, 16)
+    g.sync.dma_start(out=T.gs[:], in_=T.g[:]).then_inc(T.sem.gl, 16)
+    g.wait_ge(T.sem.zl, 16)
+    issue(g, core, T, topo, calls[core])
+
+    due = {}
+    for c in sorted(calls):
+        for need, trs in calls[c]:
+            for tr in trs:
+                if tr[3] == core:
+                    due[tr[6]] = due.get(tr[6], 0) + engines(tr[5])
+    sems = {"rx": T.sem.rx, "cx": T.sem.cx, "mt": T.sem.mt, "rs": T.sem.rs, "cs": T.sem.cs, "d0": T.sem.d0,
+            "d1": T.sem.d1}
+
+    done = [0]
+
+    def op(inst):
+        inst.then_inc(T.sem.vs, 1)
+        done[0] += 1
+
+    def settle():
+        v.wait_ge(T.sem.vs, done[0])
+
+    op(v.memset(T.yb[:], 0.0))
+    op(v.memset(T.gp[:], 0.0))
+    settle()
+    v.wait_ge(T.sem.gl, 16)
+    pairs = []
+    for e in range(n):
+        for i, (t, k) in enumerate(cols[e][rank]):
+            pairs.append((col[rank][e] + i, t * kk + k))
+    for sj, sg, js in ap_groups(pairs):
+        op(v.tensor_copy(out=T.gp[:, sj], in_=T.gs[:, sg]))
+
+    frm = {kind[e][rank]: e for e in range(n)}
+    for st in [["self"]] + STAGES:
+        lo, hi = min(span[rank][kd][0] for kd in st), max(span[rank][kd][1] for kd in st)
+        items = []
+        for kd in st:
+            e = frm[kd]
+            items += [(t, col[rank][e] + i) for i, (t, k) in enumerate(cols[e][rank])]
+            if kd == "self":
+                v.wait_ge(T.sem.zl, 16)
+            elif kd in due:
+                v.wait_ge(sems[kd], due[kd])
+        if not items:
+            continue
+        settle()
+        src = T.zs[:, off[rank][rank]:off[rank][rank] + hi - lo] if st == ["self"] else T.land[:, lo:hi]
+        op(v.tensor_tensor(out=T.prod[:, lo:hi], in0=src, in1=T.gp[:, lo:hi], op=mult))
+        settle()
+        dirty = set()
+        for s_t, s_j, ts in ap_groups(items):
+            if dirty & set(ts):
+                settle()
+                dirty = set()
+            op(v.tensor_tensor(out=T.yb[:, s_t], in0=T.yb[:, s_t], in1=T.prod[:, s_j], op=add))
+            dirty |= set(ts)
+
+    g.sync.wait_ge(T.sem.vs, done[0])
+    g.sync.dma_start(out=T.y[:], in_=T.yb[:]).then_inc(T.sem.st, 16)
+    g.sync.wait_ge(T.sem.st, 16)

@@ -1,13 +1,13 @@
 import concourse.bass as bass
 import concourse.mybir as mybir
 
-LW = 52
+LW = 48
 SCRATCH = {
     "zs": ("sbuf", [128, 40], "float32"),
     "gs": ("sbuf", [128, 32], "float32"),
     "land": ("sbuf", [128, LW], "float32"),
-    "gp": ("sbuf", [128, LW], "float32"),
-    "prod": ("sbuf", [128, LW], "float32"),
+    "zz": ("sbuf", [128, 32], "float32"),
+    "prod": ("sbuf", [128, 32], "float32"),
     "yb": ("sbuf", [128, 16], "float32"),
 }
 SEMAPHORES = ["zl", "gl", "st", "vs", "sent", "si", "rx", "cx", "mt", "rs", "cs", "d0", "d1"]
@@ -38,7 +38,7 @@ def ap_groups(items):
         else:
             da, db = best[1][0] - best[0][0], best[1][1] - best[0][1]
             sa, sb = slice(best[0][0], best[-1][0] + 1, da), slice(best[0][1], best[-1][1] + 1, db)
-        out.append((sa, sb, [p[0] for p in best]))
+        out.append((sa, sb))
         left = [p for p in left if p not in best]
     return out
 
@@ -87,17 +87,14 @@ def make_plan(tables, cores, topo):
 
     col = [[0] * n for r in range(n)]
     base = [[0] * n for r in range(n)]
-    span = [{} for r in range(n)]
     for r in range(n):
         frm = {kind[e][r]: e for e in range(n)}
-        at = cnt[r][r]
-        span[r]["self"] = (0, at)
+        at = 0
         for st in STAGES:
             for kd in st:
                 e = frm[kd]
                 ws, w = win[(e, r)]
                 base[r][e], col[r][e] = at, at + off[e][r] - ws
-                span[r][kd] = (at, at + w)
                 at += w
         assert at <= LW
 
@@ -117,7 +114,7 @@ def make_plan(tables, cores, topo):
                     (0, last("zs", 0, direct, (0x0F, 0xF0)))]
         calls[rc] = [(8, last("land", s_r, via_r, (0x0F, 0xF0, 0xFF00)))]
         calls[ac] = [(8, last("land", s_a, via_a, (0x0F, 0xF0)))]
-    return calls, cols, cnt, off, kind, col, span
+    return calls, cols, cnt, off, kind, col
 
 
 def engines(mask):
@@ -148,7 +145,7 @@ def issue(g, core, T, topo, call_list):
 
 
 def rank_program(g, core, T, topo):
-    calls, cols, cnt, off, kind, col, span = make_plan(T.tables, T.cores, topo)
+    calls, cols, cnt, off, kind, col = make_plan(T.tables, T.cores, topo)
     rank = T.rank_of(core)
     if rank is None:
         if core in calls:
@@ -181,41 +178,26 @@ def rank_program(g, core, T, topo):
     def settle():
         v.wait_ge(T.sem.vs, done[0])
 
-    op(v.memset(T.yb[:], 0.0))
-    op(v.memset(T.gp[:], 0.0))
-    settle()
-    v.wait_ge(T.sem.gl, 16)
-    pairs = []
-    for e in range(n):
-        for i, (t, k) in enumerate(cols[e][rank]):
-            pairs.append((col[rank][e] + i, t * kk + k))
-    for sj, sg, js in ap_groups(pairs):
-        op(v.tensor_copy(out=T.gp[:, sj], in_=T.gs[:, sg]))
-
     frm = {kind[e][rank]: e for e in range(n)}
     for st in [["self"]] + STAGES:
-        lo, hi = min(span[rank][kd][0] for kd in st), max(span[rank][kd][1] for kd in st)
         items = []
         for kd in st:
             e = frm[kd]
-            items += [(t, col[rank][e] + i) for i, (t, k) in enumerate(cols[e][rank])]
+            first = off[rank][rank] if kd == "self" else col[rank][e]
+            items += [(t * kk + k, first + i) for i, (t, k) in enumerate(cols[e][rank])]
             if kd == "self":
                 v.wait_ge(T.sem.zl, 16)
             elif kd in due:
                 v.wait_ge(sems[kd], due[kd])
-        if not items:
-            continue
-        settle()
-        src = T.zs[:, off[rank][rank]:off[rank][rank] + hi - lo] if st == ["self"] else T.land[:, lo:hi]
-        op(v.tensor_tensor(out=T.prod[:, lo:hi], in0=src, in1=T.gp[:, lo:hi], op=mult))
-        settle()
-        dirty = set()
-        for s_t, s_j, ts in ap_groups(items):
-            if dirty & set(ts):
-                settle()
-                dirty = set()
-            op(v.tensor_tensor(out=T.yb[:, s_t], in0=T.yb[:, s_t], in1=T.prod[:, s_j], op=add))
-            dirty |= set(ts)
+        src = T.zs if st == ["self"] else T.land
+        for s_q, s_j in ap_groups(items):
+            op(v.tensor_copy(out=T.zz[:, s_q], in_=src[:, s_j]))
+    v.wait_ge(T.sem.gl, 16)
+    settle()
+    op(v.tensor_tensor(out=T.prod[:], in0=T.zz[:], in1=T.gs[:], op=mult))
+    settle()
+    tk = len(T.tables["ROUTE"][rank]) * kk
+    op(v.tensor_tensor(out=T.yb[:], in0=T.prod[:, 0:tk:kk], in1=T.prod[:, 1:tk:kk], op=add))
 
     g.sync.wait_ge(T.sem.vs, done[0])
     g.sync.dma_start(out=T.y[:], in_=T.yb[:]).then_inc(T.sem.st, 16)

@@ -6,13 +6,12 @@ SCRATCH = {
     "zs": ("sbuf", [128, 40], "float32"),
     "gs": ("sbuf", [128, 32], "float32"),
     "land": ("sbuf", [128, LW], "float32"),
-    "zz": ("sbuf", [128, 32], "float32"),
     "prod": ("sbuf", [128, 32], "float32"),
     "yb": ("sbuf", [128, 16], "float32"),
 }
 SEMAPHORES = ["zl", "gl", "st", "vs", "sent", "si", "rx", "cx", "mt", "rs", "cs", "d0", "d1"]
 
-STAGES = [["rx", "cx"], ["mt", "rs"], ["cs"], ["d0", "d1"]]
+STAGES = [["rx", "cx"], ["mt", "rs"], ["cs"]]
 R_CORE, A_CORE = 3, 6
 
 
@@ -53,6 +52,10 @@ def kind_of(he, ce, hr, cr):
     return "d0" if ce == 0 else "d1"
 
 
+def late_kinds(chip):
+    return ["d0", "d1"] if chip % 2 == 0 else ["d1", "d0"]
+
+
 def make_plan(tables, cores, topo):
     route, zw = tables["ROUTE"], tables["ZW"]
     n = len(route)
@@ -90,7 +93,7 @@ def make_plan(tables, cores, topo):
     for r in range(n):
         frm = {kind[e][r]: e for e in range(n)}
         at = 0
-        for st in STAGES:
+        for st in STAGES + [late_kinds(place[r][1])]:
             for kd in st:
                 e = frm[kd]
                 ws, w = win[(e, r)]
@@ -179,7 +182,10 @@ def rank_program(g, core, T, topo):
         v.wait_ge(T.sem.vs, done[0])
 
     frm = {kind[e][rank]: e for e in range(n)}
-    for st in [["self"]] + STAGES:
+    late = late_kinds(topo.chip(core))
+
+    v.wait_ge(T.sem.gl, 16)
+    for st in [["self"]] + STAGES + [[kd] for kd in late]:
         items = []
         for kd in st:
             e = frm[kd]
@@ -191,10 +197,7 @@ def rank_program(g, core, T, topo):
                 v.wait_ge(sems[kd], due[kd])
         src = T.zs if st == ["self"] else T.land
         for s_q, s_j in ap_groups(items):
-            op(v.tensor_copy(out=T.zz[:, s_q], in_=src[:, s_j]))
-    v.wait_ge(T.sem.gl, 16)
-    settle()
-    op(v.tensor_tensor(out=T.prod[:], in0=T.zz[:], in1=T.gs[:], op=mult))
+            op(v.tensor_tensor(out=T.prod[:, s_q], in0=src[:, s_j], in1=T.gs[:, s_q], op=mult))
     settle()
     tk = len(T.tables["ROUTE"][rank]) * kk
     op(v.tensor_tensor(out=T.yb[:], in0=T.prod[:, 0:tk:kk], in1=T.prod[:, 1:tk:kk], op=add))

import concourse.bass as bass
import concourse.mybir as mybir

LW = 48
SCRATCH = {
    "zs": ("sbuf", [128, 40], "float32"),
    "gs": ("sbuf", [128, 32], "float32"),
    "land": ("sbuf", [128, LW], "float32"),
    "prod": ("sbuf", [128, 32], "float32"),
    "yb": ("sbuf", [128, 16], "float32"),
}
SEMAPHORES = ["zl", "gl", "st", "vs", "sent", "si", "rx", "cx", "mt", "rs", "cs", "d0", "d1"]

STAGES = [["rx", "cx"], ["mt", "rs"], ["cs"]]
R_CORE, A_CORE = 3, 6


def ap_groups(items):
    left = sorted(items)
    out = []
    while left:
        have = set(left)
        best = [left[0]]
        for p in left:
            for q in left:
                if q[0] > p[0] and q[1] > p[1]:
                    da, db = q[0] - p[0], q[1] - p[1]
                    run = [p, q]
                    nxt = (q[0] + da, q[1] + db)
                    while nxt in have:
                        run.append(nxt)
                        nxt = (nxt[0] + da, nxt[1] + db)
                    if len(run) > len(best):
                        best = run
        if len(best) == 1:
            sa, sb = slice(best[0][0], best[0][0] + 1), slice(best[0][1], best[0][1] + 1)
        else:
            da, db = best[1][0] - best[0][0], best[1][1] - best[0][1]
            sa, sb = slice(best[0][0], best[-1][0] + 1, da), slice(best[0][1], best[-1][1] + 1, db)
        out.append((sa, sb))
        left = [p for p in left if p not in best]
    return out


def kind_of(he, ce, hr, cr):
    if he == hr:
        return "self" if ce == cr else "mt"
    if hr == he ^ 1:
        return "rs" if ce == cr else "rx"
    if hr == 3 - he:
        return "cs" if ce == cr else "cx"
    return "d0" if ce == 0 else "d1"


def late_kinds(chip):
    return ["d0", "d1"] if chip % 2 == 0 else ["d1", "d0"]


def make_plan(tables, cores, topo):
    route, zw = tables["ROUTE"], tables["ZW"]
    n = len(route)
    place = [(topo.host(c), topo.chip(c)) for c in cores]
    cols = [[[] for r in range(n)] for e in range(n)]
    off = [[0] * n for e in range(n)]
    fill = [0] * n
    for r in range(n):
        for e in range(n):
            off[e][r] = fill[e]
        for t, ex in enumerate(route[r]):
            for k, e in enumerate(ex):
                cols[e][r].append((t, k))
                fill[e] += 1
    cnt = [[len(cols[e][r]) for r in range(n)] for e in range(n)]
    kind = [[kind_of(place[e][0], place[e][1], place[r][0], place[r][1]) for r in range(n)] for e in range(n)]

    win, chunk = {}, {}
    for e in range(n):
        to = {kind[e][r]: r for r in range(n)}
        dd = [r for r in range(n) if kind[e][r] in ("d0", "d1")]
        via_r, via_a, direct = dd + [to["cs"]], [to["mt"], to["rs"]], [to["rx"], to["cx"]]
        lo_r, hi_r = min(off[e][r] for r in via_r), max(off[e][r] + cnt[e][r] for r in via_r)
        lo_a, hi_a = min(off[e][r] for r in via_a), max(off[e][r] + cnt[e][r] for r in via_a)
        w1 = max(hi_r - lo_r, hi_a - lo_a)
        s_r, s_a = min(lo_r, zw - w1), min(lo_a, zw - w1)
        chunk[e] = (s_r, s_a, w1, via_r, via_a, direct)
        for grp, lo, hi in ((via_r, s_r, s_r + w1), (via_a, s_a, s_a + w1), (direct, 0, zw)):
            w = max(cnt[e][r] for r in grp)
            for r in grp:
                win[(e, r)] = (min(off[e][r], hi - w), w)

    col = [[0] * n for r in range(n)]
    base = [[0] * n for r in range(n)]
    for r in range(n):
        frm = {kind[e][r]: e for e in range(n)}
        at = 0
        for st in STAGES + [late_kinds(place[r][1])]:
            for kd in st:
                e = frm[kd]
                ws, w = win[(e, r)]
                base[r][e], col[r][e] = at, at + off[e][r] - ws
                at += w
        assert at <= LW

    calls = {}
    for e in range(n):
        s = cores[e]
        he, ce = place[e]
        rc = (3 - he) * 128 + ce * 8 + R_CORE
        ac = he * 128 + ce * 8 + A_CORE
        s_r, s_a, w1, via_r, via_a, direct = chunk[e]

        def last(buf, shift, grp, masks):
            return [(buf, win[(e, r)][0] - shift, win[(e, r)][1], cores[r], base[r][e], m, kind[e][r])
                    for r, m in zip(grp, masks) if cnt[e][r]]

        calls[s] = [(0, [("zs", s_r, w1, rc, 0, 0x00FF, "si"), ("zs", s_a, w1, ac, 0, 0xFF00, "si")]),
                    (0, last("zs", 0, direct, (0x0F, 0xF0)))]
        calls[rc] = [(8, last("land", s_r, via_r, (0x0F, 0xF0, 0xFF00)))]
        calls[ac] = [(8, last("land", s_a, via_a, (0x0F, 0xF0)))]
    return calls, cols, cnt, off, kind, col


def engines(mask):
    return bin(mask).count("1")


def issue(g, core, T, topo, call_list):
    sems = {"si": T.sem.si, "rx": T.sem.rx, "cx": T.sem.cx, "mt": T.sem.mt, "rs": T.sem.rs, "cs": T.sem.cs,
            "d0": T.sem.d0, "d1": T.sem.d1}
    bufs = {"zs": T.zs, "land": T.land}
    left = 0
    for need, trs in call_list:
        if need:
            g.wait_ge(T.sem.si, need)
        if not trs:
            continue
        lst = []
        for buf, lo, w, dst, dlo, mask, sem in trs:
            rid, pid = topo.addr(dst, core)
            assert mask & ~topo.mask(core, dst) == 0
            lst.append(bass.RemoteDMATransfer(dst_ids=[bass.DstId(rid=rid, pnc=pid)], dma_engine_mask=mask,
                                              remote_sem=sems[sem], src=bufs[buf][:, lo:lo + w],
                                              dst=T.land[:, dlo:dlo + w]))
            left += engines(mask)
        g.remote_dma_fused(lst, local_sem=T.sem.sent)
    if left:
        g.wait_ge(T.sem.sent, left)


def rank_program(g, core, T, topo):
    calls, cols, cnt, off, kind, col = make_plan(T.tables, T.cores, topo)
    rank = T.rank_of(core)
    if rank is None:
        if core in calls:
            issue(g, core, T, topo, calls[core])
        return
    n, kk, zw = len(T.cores), T.tables["K"], T.tables["ZW"]
    add, mult = mybir.AluOpType.add, mybir.AluOpType.mult
    v = g.vector

    g.sync.dma_start(out=T.zs[:, 0:zw], in_=T.z[:]).then_inc(T.sem.zl, 16)
    g.sync.dma_start(out=T.gs[:], in_=T.g[:]).then_inc(T.sem.gl, 16)
    g.wait_ge(T.sem.zl, 16)
    issue(g, core, T, topo, calls[core])

    due = {}
    for c in sorted(calls):
        for need, trs in calls[c]:
            for tr in trs:
                if tr[3] == core:
                    due[tr[6]] = due.get(tr[6], 0) + engines(tr[5])
    sems = {"rx": T.sem.rx, "cx": T.sem.cx, "mt": T.sem.mt, "rs": T.sem.rs, "cs": T.sem.cs, "d0": T.sem.d0,
            "d1": T.sem.d1}

    done = [0]

    def op(inst):
        inst.then_inc(T.sem.vs, 1)
        done[0] += 1

    def settle():
        v.wait_ge(T.sem.vs, done[0])

    frm = {kind[e][rank]: e for e in range(n)}
    late = late_kinds(topo.chip(core))

    v.wait_ge(T.sem.gl, 16)
    for st in [["self"]] + STAGES + [[kd] for kd in late]:
        items = []
        for kd in st:
            e = frm[kd]
            first = off[rank][rank] if kd == "self" else col[rank][e]
            items += [(t * kk + k, first + i) for i, (t, k) in enumerate(cols[e][rank])]
            if kd == "self":
                v.wait_ge(T.sem.zl, 16)
            elif kd in due:
                v.wait_ge(sems[kd], due[kd])
        src = T.zs if st == ["self"] else T.land
        for s_q, s_j in ap_groups(items):
            op(v.tensor_tensor(out=T.prod[:, s_q], in0=src[:, s_j], in1=T.gs[:, s_q], op=mult))
    settle()
    tk = len(T.tables["ROUTE"][rank]) * kk
    op(v.tensor_tensor(out=T.yb[:], in0=T.prod[:, 0:tk:kk], in1=T.prod[:, 1:tk:kk], op=add))

    g.sync.wait_ge(T.sem.vs, done[0])
    g.sync.dma_start(out=T.y[:], in_=T.yb[:]).then_inc(T.sem.st, 16)
    g.sync.wait_ge(T.sem.st, 16)
